import numpy as np
import ml_dtypes


def mxq(x, axis, fmt="e4m3"):
    dtype, down = {"e4m3": (ml_dtypes.float8_e4m3fn, 7), "e5m2": (ml_dtypes.float8_e5m2, 14)}[fmt]
    v = np.moveaxis(np.asarray(x, np.float32).astype(ml_dtypes.bfloat16).astype(np.float64), axis, -1)
    blocks = v.reshape(v.shape[:-1] + (-1, 32))
    amax = np.abs(blocks).max(-1, keepdims=True)
    byte = np.maximum(np.where(amax > 0, np.frexp(amax)[1] - 1 + 127, 0) - down, 1)
    scale = np.exp2(byte - 127.0)
    codes = (blocks / scale).astype(np.float32).astype(dtype).astype(np.float64)
    return np.moveaxis((codes * scale).reshape(v.shape), -1, axis)


WIDE = False


def mx_kscale(k):
    if not WIDE:
        return np.ones(k)
    levels = np.array([10, -10, 5, -5, 0])
    if k % 512:
        return np.exp2(np.random.permutation(np.resize(levels, k // 32))).repeat(32)
    a = np.empty((k // 512, 16))
    for p in range(k // 512):
        a[p, :8] = np.random.permutation(np.resize(levels, 8))
        for g in range(8):
            far = levels[np.abs(levels - a[p, g]) >= 10]
            a[p, g + 8] = far[np.random.randint(len(far))]
    return np.exp2(a.ravel()).repeat(32)


def f64(x):
    return np.asarray(x).astype(np.float64)


def striped(idx):
    return np.tile(idx.reshape(-1, 16).T, (8, 1)).astype(np.uint16)


def unstriped(offs):
    return offs[:16].T.reshape(-1).astype(np.int64)


E2M1 = np.array([0.0, 0.5, 1.0, 1.5, 2.0, 3.0, 4.0, 6.0, -0.0, -0.5, -1.0, -1.5, -2.0, -3.0, -4.0, -6.0])


def pack_weight(w, fmt):
    k, n = w.shape
    w = f64(np.asarray(w, np.float32).astype(ml_dtypes.bfloat16)).reshape(k // 32, 32, n)
    amax = np.abs(w).max(1)
    if fmt == "e4m3":
        byte = np.frexp(amax)[1] - 1 + 127 - 7
    else:
        mant, ex = np.frexp(amax / 6.0)
        byte = np.where(mant > 0.5, ex, ex - 1) + 127
    byte = np.clip(np.where(amax > 0, byte, 1), 1, 254)
    scaled = (w * np.exp2(127.0 - byte)[:, None, :]).reshape(k, n).astype(np.float32)
    by_word = np.ascontiguousarray(scaled.reshape(k // 512, 128, 4, n).transpose(0, 1, 3, 2))
    if fmt == "e4m3":
        words = by_word.astype(ml_dtypes.float8_e4m3fn).view(np.uint8)
    else:
        c = by_word.astype(ml_dtypes.float4_e2m1fn).view(np.uint8) & 0xF
        words = (c[..., 0::2] | (c[..., 1::2] << 4)).reshape(k // 512, 128, 2 * n)
    return np.ascontiguousarray(words), np.ascontiguousarray(byte.astype(np.uint8).reshape(k // 512, 16, n))


def unpack_weight(words, scales, fmt):
    g, _, n = scales.shape
    words = np.ascontiguousarray(words).reshape(g, 128, n, -1)
    if fmt == "e4m3":
        vals = words.view(ml_dtypes.float8_e4m3fn).astype(np.float64)
    else:
        nib = np.empty((g, 128, n, 4), np.uint8)
        nib[..., 0::2] = words & 0xF
        nib[..., 1::2] = words >> 4
        vals = E2M1[nib]
    vals = vals * np.repeat(np.exp2(scales.astype(np.float64) - 127.0), 8, axis=1)[..., None]
    return vals.transpose(0, 1, 3, 2).reshape(g * 512, n)


def gelu(v):
    return 0.5 * v * (1.0 + np.tanh(np.sqrt(2.0 / np.pi) * (v + 0.044715 * v**3)))


K, M, H, T, S, T2, S2, T3, P = 1536, 512, 512, 4096, 1024, 2048, 1024, 4096, 512

def setup_inputs():
    n = np.random.standard_normal
    s = mx_kscale(K)[:, None]
    s2 = mx_kscale(M)[:, None]
    u = mx_kscale(H)[:, None]
    tab_words, tab_scales = pack_weight(n((K, T)) * s, "e4m3")
    tok_words, tok_scales = pack_weight(n((M, S)) * s2, "e4m3")
    w4_words, w4_scales = pack_weight(n((M, H)) * 0.7 / np.sqrt(M) / s2 * u.T, "e2m1")
    tab2_words, tab2_scales = pack_weight(n((H, T3)) * 1.5 / np.sqrt(H) / u, "e4m3")
    return {
        "tab_words": tab_words, "tab_scales": tab_scales,
        "offs": striped(np.random.permutation(T)[:S]),
        "tab2_words": tab2_words, "tab2_scales": tab2_scales,
        "offs2": striped(np.random.permutation(T3)[:S2]),
        "offs3": striped(np.random.permutation(T2)[:S]),
        "offs4": striped(np.random.permutation(T2)[:P]),
        "tok_words": tok_words, "tok_scales": tok_scales,
        "w4_words": w4_words, "w4_scales": w4_scales,
        "w1": (n((K, H)) * 0.75 / np.sqrt(K) / s * u.T).astype(np.float32),
        "wgs": np.exp(0.3 * n((128, S))).astype(np.float32),
        "page0": (n((H, T2)) * u).astype(np.float32),
        "lim": (np.random.uniform(-0.2, 0.8, H) * u[:, 0]).astype(np.float32),
        "fit": np.exp(0.4 * n((S2, P))).astype(np.float32),
    }

def reference(tab_words, tab_scales, offs, tab2_words, tab2_scales, offs2, offs3, offs4,
              tok_words, tok_scales, w4_words, w4_scales, w1, wgs, page0, lim, fit):
    v = unpack_weight(tab_words, tab_scales, "e4m3")[:, unstriped(offs)]
    v2 = unpack_weight(tab2_words, tab2_scales, "e4m3")[:, unstriped(offs2)]
    tok = unpack_weight(tok_words, tok_scales, "e4m3")
    w4 = unpack_weight(w4_words, w4_scales, "e2m1")
    h = mxq(f64(w1), 0, "e4m3").T @ v + w4.T @ tok
    page = f64(page0).copy()
    page[:, unstriped(offs3)] = np.tile(f64(wgs), (H // 128, 1)) * h
    x = np.minimum(page[:, unstriped(offs4)], f64(lim)[:, None])
    e = v2.T @ mxq(x, 0, "e4m3")
    return np.tanh(e) * f64(fit)

@@ -1,0 +1,218 @@
+from contextlib import ExitStack
+
+import concourse.mybir as mybir
+
+K, M, H, T, S, T2, S2, T3, CTX = 1536, 512, 512, 4096, 1024, 2048, 1024, 4096, 512
+FLOPS = 2 * (K + M) * H * S + 2 * H * S2 * CTX
+
+F32 = mybir.dt.float32
+BF16 = mybir.dt.bfloat16
+I32 = mybir.dt.int32
+U32 = mybir.dt.uint32
+U16 = mybir.dt.uint16
+U8 = mybir.dt.uint8
+FP8X4 = mybir.dt.float8_e4m3fn_x4
+FP4X4 = mybir.dt.float4_e2m1fn_x4
+MULT = mybir.AluOpType.mult
+MIN = mybir.AluOpType.min
+TANH = mybir.ActivationFunctionType.Tanh
+
+P = 128
+PACK = 4
+QUADS = 4
+QUAD = P // QUADS
+K_PASS = P * PACK
+PASSES = K // K_PASS
+BLOCKS = H // P
+BANK = 512
+LANES = 16
+W_COLS = H // 2
+
+
+def tile_list_completion_popup_scores_kernel(
+    tc, tab_words, tab_scales, offs, tab2_words, tab2_scales, offs2, offs3, offs4,
+    tok_words, tok_scales, w4_words, w4_scales, w1, wgs, page0, lim, fit, out,
+):
+    nc = tc.nc
+
+    def words_of(dram, a):
+        return dram[a].rearrange("p n t -> p (n t)").bitcast(I32)
+
+    with ExitStack() as ctx:
+        keep = ctx.enter_context(tc.tile_pool(name="keep", bufs=1))
+        ring = ctx.enter_context(tc.tile_pool(name="ring", bufs=4))
+        psum = ctx.enter_context(tc.psum_pool(name="psum", bufs=8))
+
+        def load_list(dram, name):
+            tile = keep.tile(list(dram.shape), U16, name=name)
+            nc.sync.dma_start(tile[:], dram)
+            return tile
+
+        def load_scale_rows(queue, plane, dram):
+            passes = dram.shape[0]
+            for q in range(QUADS):
+                rows = slice(QUAD * q, QUAD * q + 4 * passes)
+                queue.dma_start(plane[rows, :].bitcast(I32), dram[:, 4 * q : 4 * q + 4, :].bitcast(I32))
+
+        tab_plane = keep.tile([P, T], U8, align_bytes=64)
+        tab2_plane = keep.tile([P, T3], U8, align_bytes=64)
+        for plane, dram in ((tab_plane, tab_scales), (tab2_plane, tab2_scales)):
+            nc.vector.memset(plane[:].bitcast(I32), 0)
+            load_scale_rows(nc.gpsimd, plane, dram)
+        tok_plane = keep.tile([P, S], U8, align_bytes=64)
+        w4_plane = keep.tile([P, H], U8, align_bytes=64)
+        load_scale_rows(nc.scalar, tok_plane, tok_scales)
+        load_scale_rows(nc.scalar, w4_plane, w4_scales)
+
+        def load_w1(half):
+            raws = []
+            for a in range(PASSES):
+                raw = keep.tile([P, PACK, W_COLS], F32, name=f"w1_raw{half}{a}")
+                rows = w1[a * K_PASS : (a + 1) * K_PASS, half * W_COLS : (half + 1) * W_COLS]
+                nc.sync.dma_start(raw[:], rows.rearrange("(p t) c -> p t c", t=PACK))
+                raws.append(raw)
+            return raws
+
+        def load_page(b):
+            tile = keep.tile([P, T2], F32, name=f"page{b}")
+            nc.sync.dma_start(tile[:], page0[b * P : (b + 1) * P, :])
+            return tile
+
+        list1 = load_list(offs, "list1")
+        list2 = load_list(offs2, "list2")
+        w1_raw = [load_w1(0)]
+        w4_sb = keep.tile([P, 2 * H], U8, align_bytes=64)
+        nc.sync.dma_start(w4_sb[:].bitcast(I32), w4_words[0].bitcast(I32))
+        tok_sb = keep.tile([P, S], U32, align_bytes=64)
+        tok_dram = words_of(tok_words, 0)
+        nc.sync.dma_start(tok_sb[:, :BANK].bitcast(I32), tok_dram[:, :BANK])
+        tab_sb = []
+        for a in range(PASSES):
+            tile = keep.tile([P, T], U32, name=f"tab{a}")
+            nc.sync.dma_start(tile[:].bitcast(I32), words_of(tab_words, a))
+            tab_sb.append(tile)
+        list3 = load_list(offs3, "list3")
+        wgs_sb = keep.tile([P, S], F32)
+        nc.sync.dma_start(wgs_sb[:, :BANK], wgs[:, :BANK])
+        page = [load_page(0)]
+        nc.sync.dma_start(tok_sb[:, BANK:].bitcast(I32), tok_dram[:, BANK:])
+        nc.sync.dma_start(wgs_sb[:, BANK:], wgs[:, BANK:])
+        list4 = load_list(offs4, "list4")
+        lim_sb = keep.tile([P, BLOCKS], F32)
+        with nc.allow_non_contiguous_dma(reason="one ceiling for each partition and row block"):
+            nc.sync.dma_start(lim_sb[:], lim.rearrange("(b p) -> p b", p=P))
+        w1_raw.append(load_w1(1))
+        for b in range(1, BLOCKS):
+            page.append(load_page(b))
+        tab2_sb = keep.tile([P, T3], U32)
+        nc.sync.dma_start(tab2_sb[:].bitcast(I32), words_of(tab2_words, 0))
+        fit_sb = []
+        for half in range(2):
+            tile = keep.tile([P, 4, CTX], F32, name=f"fit{half}")
+            rows = fit[half * 4 * P : (half + 1) * 4 * P, :]
+            nc.sync.dma_start(tile[:], rows.rearrange("(c p) j -> p c j", p=P))
+            fit_sb.append(tile)
+
+        def quantise_w1(half):
+            made = []
+            for a in range(PASSES):
+                woven = ring.tile([P, W_COLS, PACK], BF16, name="w1_woven", bufs=3, align_bytes=64)
+                nc.scalar.copy(woven[:], w1_raw[half][a][:].rearrange("p t c -> p c t"))
+                codes = keep.tile([P, W_COLS], U32, name=f"w1_codes{half}{a}", align_bytes=64)
+                plane = keep.tile([P, W_COLS], U8, name=f"w1_plane{half}{a}", align_bytes=64)
+                nc.vector.quantize_mx(
+                    out=codes[:].bitcast(FP8X4), scales=plane[:],
+                    in_=woven[:].rearrange("p c t -> p (c t)"),
+                )
+                made.append((codes, plane))
+            return made
+
+        w1_q = [quantise_w1(0)]
+
+        v_plane = keep.tile([P, S], U8, align_bytes=64)
+        nc.vector.tensor_copy(v_plane[:], tab_plane[:].indirect(list1[:]))
+        v2_plane = keep.tile([P, S2], U8, align_bytes=64)
+        nc.vector.tensor_copy(v2_plane[:], tab2_plane[:].indirect(list2[:]))
+        v_words = []
+        for a in range(PASSES):
+            tile = keep.tile([P, S], U32, name=f"v_words{a}", align_bytes=64)
+            step = BANK if a == PASSES - 1 else S
+            for j0 in range(0, S, step):
+                picks = list1[:, j0 // LANES : (j0 + step) // LANES]
+                nc.vector.tensor_copy(tile[:, j0 : j0 + step], tab_sb[a][:].indirect(picks))
+            v_words.append(tile)
+
+        w1_q.append(quantise_w1(1))
+
+        x_planes = keep.tile([P, PACK, CTX], BF16)
+        for b in range(BLOCKS):
+            half, c0 = divmod(b * P, W_COLS)
+            h_sb = keep.tile([P, S], F32, name=f"h{b}")
+            for j0 in range(0, S, BANK):
+                cols = slice(j0, j0 + BANK)
+                tok_pass = (
+                    w4_sb[:, 2 * b * P : 2 * (b + 1) * P].bitcast(FP4X4), w4_plane[:, b * P : (b + 1) * P],
+                    tok_sb[:, cols].bitcast(FP8X4), tok_plane[:, cols],
+                )
+                tab_passes = [
+                    (
+                        w1_q[half][a][0][:, c0 : c0 + P].bitcast(FP8X4), w1_q[half][a][1][:, c0 : c0 + P],
+                        v_words[a][:, cols].bitcast(FP8X4), v_plane[4 * a :, cols],
+                    )
+                    for a in range(PASSES)
+                ]
+                passes = [tok_pass] + tab_passes if j0 == 0 else tab_passes + [tok_pass]
+                acc = psum.tile([P, BANK], F32, name="acc")
+                for n, (lhs, lhs_scale, rhs, rhs_scale) in enumerate(passes):
+                    nc.tensor.matmul_mx(
+                        out=acc[:], lhsT=lhs, lhsT_scale=lhs_scale, rhs=rhs, rhs_scale=rhs_scale,
+                        start=(n == 0), stop=(n == len(passes) - 1),
+                    )
+                nc.scalar.copy(h_sb[:, cols], acc[:])
+            step = BANK if b == 0 else S
+            for j0 in range(0, S, step):
+                places = list3[:, j0 // LANES : (j0 + step) // LANES]
+                nc.vector.tensor_tensor(
+                    page[b][:].indirect(places), h_sb[:, j0 : j0 + step], wgs_sb[:, j0 : j0 + step], MULT
+                )
+            picked = keep.tile([P, CTX], F32, name="picked", tag="picked", align_bytes=64)
+            nc.vector.tensor_copy(picked[:], page[b][:].indirect(list4[:]))
+            x_rows = keep.tile([P, CTX], BF16, name=f"x_rows{b}")
+            nc.vector.tensor_scalar(x_rows[:], picked[:], lim_sb[:, b : b + 1], None, MIN)
+            queue = nc.sync if b == BLOCKS - 1 else nc.gpsimd
+            queue.dma_start(x_planes[QUAD * b : QUAD * (b + 1), :, :], x_rows[:])
+
+        def gather_candidates(half, tag):
+            tile = keep.tile([P, BANK], U32, name=f"v2_words{half}", tag=tag, align_bytes=64)
+            picks = list2[:, half * BANK // LANES : (half + 1) * BANK // LANES]
+            nc.vector.tensor_copy(tile[:], tab2_sb[:].indirect(picks))
+            return tile
+
+        v2_words = [gather_candidates(0, "picked")]
+        x_woven = keep.tile([P, CTX, PACK], BF16, tag="woven", align_bytes=64)
+        nc.vector.tensor_copy(
+            x_woven[:].rearrange("p (c i) t -> p c t i", i=4),
+            x_planes[:].rearrange("p t (c i) -> p c t i", i=4),
+        )
+        x_codes = keep.tile([P, CTX], U32, align_bytes=64)
+        x_plane = keep.tile([P, CTX], U8, align_bytes=64)
+        nc.vector.quantize_mx(
+            out=x_codes[:].bitcast(FP8X4), scales=x_plane[:],
+            in_=x_woven[:].rearrange("p c t -> p (c t)"),
+        )
+        v2_words.append(gather_candidates(1, "woven"))
+
+        for c in range(S2 // P):
+            half, u = divmod(c, 4)
+            acc = psum.tile([P, BANK], F32, name="acc")
+            nc.tensor.matmul_mx(
+                out=acc[:],
+                lhsT=v2_words[half][:, u * P : (u + 1) * P].bitcast(FP8X4),
+                lhsT_scale=v2_plane[:, c * P : (c + 1) * P],
+                rhs=x_codes[:].bitcast(FP8X4), rhs_scale=x_plane[:],
+                start=True, stop=True,
+            )
+            score = ring.tile([P, CTX], F32, name="score")
+            nc.scalar.activation(score[:], acc[:], TANH)
+            nc.vector.tensor_tensor(fit_sb[half][:, u, :], score[:], fit_sb[half][:, u, :], MULT)
+            nc.sync.dma_start(out[c * P : (c + 1) * P, :], fit_sb[half][:, u, :])

@@ -54,8 +54,8 @@ def tile_list_completion_popup_scores_kernel(
                 rows = slice(QUAD * q, QUAD * q + 4 * passes)
                 queue.dma_start(plane[rows, :].bitcast(I32), dram[:, 4 * q : 4 * q + 4, :].bitcast(I32))
 
-        tab_plane = keep.tile([P, T], U8, align_bytes=64)
-        tab2_plane = keep.tile([P, T3], U8, align_bytes=64)
+        tab_plane = keep.tile([P, T], U8, tag="chain0", align_bytes=64)
+        tab2_plane = keep.tile([P, T3], U8, tag="chain2", align_bytes=64)
         for plane, dram in ((tab_plane, tab_scales), (tab2_plane, tab2_scales)):
             nc.vector.memset(plane[:].bitcast(I32), 0)
             load_scale_rows(nc.gpsimd, plane, dram)
@@ -88,7 +88,7 @@ def tile_list_completion_popup_scores_kernel(
         nc.sync.dma_start(tok_sb[:, :BANK].bitcast(I32), tok_dram[:, :BANK])
         tab_sb = []
         for a in range(PASSES):
-            tile = keep.tile([P, T], U32, name=f"tab{a}")
+            tile = keep.tile([P, T], U32, name=f"tab{a}", tag=f"tab{a}", align_bytes=64)
             nc.sync.dma_start(tile[:].bitcast(I32), words_of(tab_words, a))
             tab_sb.append(tile)
         list3 = load_list(offs3, "list3")
@@ -97,12 +97,13 @@ def tile_list_completion_popup_scores_kernel(
         page = [load_page(0)]
         nc.sync.dma_start(tok_sb[:, BANK:].bitcast(I32), tok_dram[:, BANK:])
         nc.sync.dma_start(wgs_sb[:, BANK:], wgs[:, BANK:])
+        page.append(load_page(1))
+        w1_raw.append(load_w1(1))
         list4 = load_list(offs4, "list4")
         lim_sb = keep.tile([P, BLOCKS], F32)
         with nc.allow_non_contiguous_dma(reason="one ceiling for each partition and row block"):
             nc.sync.dma_start(lim_sb[:], lim.rearrange("(b p) -> p b", p=P))
-        w1_raw.append(load_w1(1))
-        for b in range(1, BLOCKS):
+        for b in range(2, BLOCKS):
             page.append(load_page(b))
         tab2_sb = keep.tile([P, T3], U32)
         nc.sync.dma_start(tab2_sb[:].bitcast(I32), words_of(tab2_words, 0))
@@ -113,74 +114,92 @@ def tile_list_completion_popup_scores_kernel(
             nc.sync.dma_start(tile[:], rows.rearrange("(c p) j -> p c j", p=P))
             fit_sb.append(tile)
 
-        def quantise_w1(half):
+        def quantise_w1(half, tag):
             made = []
+            all_woven = keep.tile([P, PASSES, W_COLS, PACK], BF16, name=f"w1_woven{half}", tag=tag, align_bytes=64)
             for a in range(PASSES):
-                woven = ring.tile([P, W_COLS, PACK], BF16, name="w1_woven", bufs=3, align_bytes=64)
-                nc.scalar.copy(woven[:], w1_raw[half][a][:].rearrange("p t c -> p c t"))
+                woven = all_woven[:, a, :, :]
+                nc.scalar.copy(woven, w1_raw[half][a][:].rearrange("p t c -> p c t"))
                 codes = keep.tile([P, W_COLS], U32, name=f"w1_codes{half}{a}", align_bytes=64)
                 plane = keep.tile([P, W_COLS], U8, name=f"w1_plane{half}{a}", align_bytes=64)
                 nc.vector.quantize_mx(
                     out=codes[:].bitcast(FP8X4), scales=plane[:],
-                    in_=woven[:].rearrange("p c t -> p (c t)"),
+                    in_=woven.rearrange("p c t -> p (c t)"),
                 )
                 made.append((codes, plane))
             return made
 
-        w1_q = [quantise_w1(0)]
+        w1_q = [quantise_w1(0, "w1_woven")]
 
         v_plane = keep.tile([P, S], U8, align_bytes=64)
         nc.vector.tensor_copy(v_plane[:], tab_plane[:].indirect(list1[:]))
-        v2_plane = keep.tile([P, S2], U8, align_bytes=64)
-        nc.vector.tensor_copy(v2_plane[:], tab2_plane[:].indirect(list2[:]))
-        v_words = []
-        for a in range(PASSES):
-            tile = keep.tile([P, S], U32, name=f"v_words{a}", align_bytes=64)
-            step = BANK if a == PASSES - 1 else S
+        def gather_words(a, tag, step):
+            tile = keep.tile([P, S], U32, name=f"v_words{a}", tag=tag, align_bytes=64)
             for j0 in range(0, S, step):
                 picks = list1[:, j0 // LANES : (j0 + step) // LANES]
                 nc.vector.tensor_copy(tile[:, j0 : j0 + step], tab_sb[a][:].indirect(picks))
-            v_words.append(tile)
+            return tile
 
-        w1_q.append(quantise_w1(1))
+        v_words = [gather_words(0, "chain0", S)]
+        v2_plane = keep.tile([P, S2], U8, tag="tab0", align_bytes=64)
+        nc.vector.tensor_copy(v2_plane[:], tab2_plane[:].indirect(list2[:]))
+        v_words.append(gather_words(1, "chain2", S))
+        v_words.append(gather_words(2, "tab1", BANK))
 
         x_planes = keep.tile([P, PACK, CTX], BF16)
-        for b in range(BLOCKS):
+
+        def first_stage(b, j0, h_part):
             half, c0 = divmod(b * P, W_COLS)
+            cols = slice(j0, j0 + BANK)
+            tok_pass = (
+                w4_sb[:, 2 * b * P : 2 * (b + 1) * P].bitcast(FP4X4), w4_plane[:, b * P : (b + 1) * P],
+                tok_sb[:, cols].bitcast(FP8X4), tok_plane[:, cols],
+            )
+            tab_passes = [
+                (
+                    w1_q[half][a][0][:, c0 : c0 + P].bitcast(FP8X4), w1_q[half][a][1][:, c0 : c0 + P],
+                    v_words[a][:, cols].bitcast(FP8X4), v_plane[4 * a :, cols],
+                )
+                for a in range(PASSES)
+            ]
+            passes = [tok_pass] + tab_passes if j0 == 0 else tab_passes + [tok_pass]
+            acc = psum.tile([P, BANK], F32, name="acc")
+            for n, (lhs, lhs_scale, rhs, rhs_scale) in enumerate(passes):
+                nc.tensor.matmul_mx(
+                    out=acc[:], lhsT=lhs, lhsT_scale=lhs_scale, rhs=rhs, rhs_scale=rhs_scale,
+                    start=(n == 0), stop=(n == len(passes) - 1),
+                )
+            nc.scalar.copy(h_part, acc[:])
+
+        def put(b, j0, h_part):
+            width = h_part.shape[1]
+            places = list3[:, j0 // LANES : (j0 + width) // LANES]
+            nc.vector.tensor_tensor(page[b][:].indirect(places), h_part, wgs_sb[:, j0 : j0 + width], MULT)
+
+        def replace_columns(b):
             h_sb = keep.tile([P, S], F32, name=f"h{b}")
             for j0 in range(0, S, BANK):
-                cols = slice(j0, j0 + BANK)
-                tok_pass = (
-                    w4_sb[:, 2 * b * P : 2 * (b + 1) * P].bitcast(FP4X4), w4_plane[:, b * P : (b + 1) * P],
-                    tok_sb[:, cols].bitcast(FP8X4), tok_plane[:, cols],
-                )
-                tab_passes = [
-                    (
-                        w1_q[half][a][0][:, c0 : c0 + P].bitcast(FP8X4), w1_q[half][a][1][:, c0 : c0 + P],
-                        v_words[a][:, cols].bitcast(FP8X4), v_plane[4 * a :, cols],
-                    )
-                    for a in range(PASSES)
-                ]
-                passes = [tok_pass] + tab_passes if j0 == 0 else tab_passes + [tok_pass]
-                acc = psum.tile([P, BANK], F32, name="acc")
-                for n, (lhs, lhs_scale, rhs, rhs_scale) in enumerate(passes):
-                    nc.tensor.matmul_mx(
-                        out=acc[:], lhsT=lhs, lhsT_scale=lhs_scale, rhs=rhs, rhs_scale=rhs_scale,
-                        start=(n == 0), stop=(n == len(passes) - 1),
-                    )
-                nc.scalar.copy(h_sb[:, cols], acc[:])
-            step = BANK if b == 0 else S
-            for j0 in range(0, S, step):
-                places = list3[:, j0 // LANES : (j0 + step) // LANES]
-                nc.vector.tensor_tensor(
-                    page[b][:].indirect(places), h_sb[:, j0 : j0 + step], wgs_sb[:, j0 : j0 + step], MULT
-                )
-            picked = keep.tile([P, CTX], F32, name="picked", tag="picked", align_bytes=64)
+                first_stage(b, j0, h_sb[:, j0 : j0 + BANK])
+            put(b, 0, h_sb[:])
+
+        def fetch_contexts(b):
+            picked = keep.tile([P, CTX], F32, name="picked", tag="chain4", align_bytes=64)
             nc.vector.tensor_copy(picked[:], page[b][:].indirect(list4[:]))
             x_rows = keep.tile([P, CTX], BF16, name=f"x_rows{b}")
             nc.vector.tensor_scalar(x_rows[:], picked[:], lim_sb[:, b : b + 1], None, MIN)
-            queue = nc.sync if b == BLOCKS - 1 else nc.gpsimd
-            queue.dma_start(x_planes[QUAD * b : QUAD * (b + 1), :, :], x_rows[:])
+            nc.sync.dma_start(x_planes[QUAD * b : QUAD * (b + 1), :, :], x_rows[:])
+
+        for j0, tag in ((0, "h0_first"), (BANK, "chain4")):
+            h_part = keep.tile([P, BANK], F32, name=f"h0_{j0}", tag=tag, align_bytes=64)
+            first_stage(0, j0, h_part[:])
+            put(0, j0, h_part[:])
+        replace_columns(1)
+        w1_q.append(quantise_w1(1, "chain4"))
+        fetch_contexts(0)
+        fetch_contexts(1)
+        for b in range(2, BLOCKS):
+            replace_columns(b)
+            fetch_contexts(b)
 
         def gather_candidates(half, tag):
             tile = keep.tile([P, BANK], U32, name=f"v2_words{half}", tag=tag, align_bytes=64)
@@ -188,7 +207,7 @@ def tile_list_completion_popup_scores_kernel(
             nc.vector.tensor_copy(tile[:], tab2_sb[:].indirect(picks))
             return tile
 
-        v2_words = [gather_candidates(0, "picked")]
+        v2_words = [gather_candidates(0, "chain4")]
         x_woven = keep.tile([P, CTX, PACK], BF16, tag="woven", align_bytes=64)
         nc.vector.tensor_copy(
             x_woven[:].rearrange("p (c i) t -> p c t i", i=4),

@@ -27,6 +27,9 @@ BLOCKS = H // P
 BANK = 512
 LANES = 16
 W_COLS = H // 2
+WEAVE_SPLIT = 368
+ROWS_BYTES = 2 * CTX
+H_BYTES = 4 * S
 
 
 def tile_list_completion_popup_scores_kernel(
@@ -41,28 +44,28 @@ def tile_list_completion_popup_scores_kernel(
     with ExitStack() as ctx:
         keep = ctx.enter_context(tc.tile_pool(name="keep", bufs=1))
         ring = ctx.enter_context(tc.tile_pool(name="ring", bufs=4))
-        psum = ctx.enter_context(tc.psum_pool(name="psum", bufs=8))
+        relay = ctx.enter_context(tc.tile_pool(name="relay", bufs=1))
+        psum = ctx.enter_context(tc.psum_pool(name="psum", bufs=1))
 
         def load_list(dram, name):
             tile = keep.tile(list(dram.shape), U16, name=name)
             nc.sync.dma_start(tile[:], dram)
             return tile
 
-        def load_scale_rows(queue, plane, dram):
-            passes = dram.shape[0]
-            for q in range(QUADS):
-                rows = slice(QUAD * q, QUAD * q + 4 * passes)
-                queue.dma_start(plane[rows, :].bitcast(I32), dram[:, 4 * q : 4 * q + 4, :].bitcast(I32))
+        def load_scale_rows(plane, dram):
+            for r in range(4):
+                nc.sync.dma_start(plane[r::QUAD, :].bitcast(I32), dram[0, r::4, :].bitcast(I32))
 
-        tab_plane = keep.tile([P, T], U8, tag="chain0", align_bytes=64)
-        tab2_plane = keep.tile([P, T3], U8, tag="chain2", align_bytes=64)
-        for plane, dram in ((tab_plane, tab_scales), (tab2_plane, tab2_scales)):
-            nc.vector.memset(plane[:].bitcast(I32), 0)
-            load_scale_rows(nc.gpsimd, plane, dram)
-        tok_plane = keep.tile([P, S], U8, align_bytes=64)
-        w4_plane = keep.tile([P, H], U8, align_bytes=64)
-        load_scale_rows(nc.scalar, tok_plane, tok_scales)
-        load_scale_rows(nc.scalar, w4_plane, w4_scales)
+        def load_packed_scale_rows(plane, dram):
+            for q in (0, 2, 1, 3):
+                rows = slice(QUAD * q, QUAD * q + 4 * PASSES)
+                nc.gpsimd.dma_start(plane[rows, :].bitcast(I32), dram[:, 4 * q : 4 * q + 4, :].bitcast(I32))
+
+        tab_plane = keep.tile([P, T], U8, tag="chain3", align_bytes=64)
+        nc.gpsimd.memset(tab_plane[:].bitcast(I32), 0)
+        load_packed_scale_rows(tab_plane, tab_scales)
+        tab2_plane = keep.tile([P, T3], U8, tag="chain1", align_bytes=64)
+        nc.vector.memset(tab2_plane[:].bitcast(I32), 0)
 
         def load_w1(half):
             raws = []
@@ -78,28 +81,41 @@ def tile_list_completion_popup_scores_kernel(
             nc.sync.dma_start(tile[:], page0[b * P : (b + 1) * P, :])
             return tile
 
-        list1 = load_list(offs, "list1")
-        list2 = load_list(offs2, "list2")
+        def table_tile(a):
+            return keep.tile([P, T], U32, name=f"tab{a}", tag=f"tab{a}", align_bytes=64)
+
+        def load_table(a, c0, c1):
+            nc.sync.dma_start(tab_sb[a][:, c0:c1].bitcast(I32), words_of(tab_words, a)[:, c0:c1])
+
+        def load_tok(part):
+            tile = keep.tile([P, BANK], U32, name=f"tok{part}", align_bytes=64)
+            nc.sync.dma_start(tile[:].bitcast(I32), words_of(tok_words, 0)[:, part * BANK : (part + 1) * BANK])
+            return tile
+
+        tab_sb = [table_tile(a) for a in range(PASSES)]
         w1_raw = [load_w1(0)]
+        list1 = load_list(offs, "list1")
+        tok_plane = keep.tile([P, S], U8, align_bytes=64)
+        load_scale_rows(tok_plane, tok_scales)
+        load_table(0, 0, T)
+        list2 = load_list(offs2, "list2")
+        list3 = load_list(offs3, "list3")
+        load_scale_rows(tab2_plane, tab2_scales)
+        load_table(1, 0, T)
+        w4_plane = keep.tile([P, H], U8, align_bytes=64)
+        load_scale_rows(w4_plane, w4_scales)
+        load_table(2, 0, T)
         w4_sb = keep.tile([P, 2 * H], U8, align_bytes=64)
         nc.sync.dma_start(w4_sb[:].bitcast(I32), w4_words[0].bitcast(I32))
-        tok_sb = keep.tile([P, S], U32, align_bytes=64)
-        tok_dram = words_of(tok_words, 0)
-        nc.sync.dma_start(tok_sb[:, :BANK].bitcast(I32), tok_dram[:, :BANK])
-        tab_sb = []
-        for a in range(PASSES):
-            tile = keep.tile([P, T], U32, name=f"tab{a}", tag=f"tab{a}", align_bytes=64)
-            nc.sync.dma_start(tile[:].bitcast(I32), words_of(tab_words, a))
-            tab_sb.append(tile)
-        list3 = load_list(offs3, "list3")
+        tok_sb = [load_tok(0)]
         wgs_sb = keep.tile([P, S], F32)
         nc.sync.dma_start(wgs_sb[:, :BANK], wgs[:, :BANK])
         page = [load_page(0)]
-        nc.sync.dma_start(tok_sb[:, BANK:].bitcast(I32), tok_dram[:, BANK:])
+        tok_sb.append(load_tok(1))
         nc.sync.dma_start(wgs_sb[:, BANK:], wgs[:, BANK:])
-        page.append(load_page(1))
         w1_raw.append(load_w1(1))
         list4 = load_list(offs4, "list4")
+        page.append(load_page(1))
         lim_sb = keep.tile([P, BLOCKS], F32)
         with nc.allow_non_contiguous_dma(reason="one ceiling for each partition and row block"):
             nc.sync.dma_start(lim_sb[:], lim.rearrange("(b p) -> p b", p=P))
@@ -114,37 +130,40 @@ def tile_list_completion_popup_scores_kernel(
             nc.sync.dma_start(tile[:], rows.rearrange("(c p) j -> p c j", p=P))
             fit_sb.append(tile)
 
-        def quantise_w1(half, tag):
+        def quantise_w1(half, wovens):
             made = []
-            all_woven = keep.tile([P, PASSES, W_COLS, PACK], BF16, name=f"w1_woven{half}", tag=tag, align_bytes=64)
-            for a in range(PASSES):
-                woven = all_woven[:, a, :, :]
-                nc.scalar.copy(woven, w1_raw[half][a][:].rearrange("p t c -> p c t"))
+            for a, woven in enumerate(wovens):
+                nc.scalar.copy(woven[:], w1_raw[half][a][:].rearrange("p t c -> p c t"))
                 codes = keep.tile([P, W_COLS], U32, name=f"w1_codes{half}{a}", align_bytes=64)
                 plane = keep.tile([P, W_COLS], U8, name=f"w1_plane{half}{a}", align_bytes=64)
                 nc.vector.quantize_mx(
                     out=codes[:].bitcast(FP8X4), scales=plane[:],
-                    in_=woven.rearrange("p c t -> p (c t)"),
+                    in_=woven[:].rearrange("p c t -> p (c t)"),
                 )
                 made.append((codes, plane))
             return made
 
-        w1_q = [quantise_w1(0, "w1_woven")]
+        def woven_tile(tag):
+            return keep.tile([P, W_COLS, PACK], BF16, name="w1_woven", tag=tag, align_bytes=64)
 
-        v_plane = keep.tile([P, S], U8, align_bytes=64)
-        nc.vector.tensor_copy(v_plane[:], tab_plane[:].indirect(list1[:]))
-        def gather_words(a, tag, step):
+        w1_q = [quantise_w1(0, [woven_tile(tag) for tag in ("woven_a", "woven_b", "woven_c")])]
+
+        def gather_words(a, step, tag):
             tile = keep.tile([P, S], U32, name=f"v_words{a}", tag=tag, align_bytes=64)
             for j0 in range(0, S, step):
                 picks = list1[:, j0 // LANES : (j0 + step) // LANES]
                 nc.vector.tensor_copy(tile[:, j0 : j0 + step], tab_sb[a][:].indirect(picks))
             return tile
 
-        v_words = [gather_words(0, "chain0", S)]
+        v_words = [gather_words(0, S, "v_words0")]
         v2_plane = keep.tile([P, S2], U8, tag="tab0", align_bytes=64)
         nc.vector.tensor_copy(v2_plane[:], tab2_plane[:].indirect(list2[:]))
-        v_words.append(gather_words(1, "chain2", S))
-        v_words.append(gather_words(2, "tab1", BANK))
+        v_words.append(gather_words(1, S, "chain1"))
+        v_plane = keep.tile([P, S], U8, tag="tab1", align_bytes=64)
+        for j0 in range(0, S, BANK):
+            picks = list1[:, j0 // LANES : (j0 + BANK) // LANES]
+            nc.vector.tensor_copy(v_plane[:, j0 : j0 + BANK], tab_plane[:].indirect(picks))
+        v_words.append(gather_words(2, BANK, "chain3"))
 
         x_planes = keep.tile([P, PACK, CTX], BF16)
 
@@ -153,7 +172,7 @@ def tile_list_completion_popup_scores_kernel(
             cols = slice(j0, j0 + BANK)
             tok_pass = (
                 w4_sb[:, 2 * b * P : 2 * (b + 1) * P].bitcast(FP4X4), w4_plane[:, b * P : (b + 1) * P],
-                tok_sb[:, cols].bitcast(FP8X4), tok_plane[:, cols],
+                tok_sb[j0 // BANK][:].bitcast(FP8X4), tok_plane[:, cols],
             )
             tab_passes = [
                 (
@@ -162,8 +181,8 @@ def tile_list_completion_popup_scores_kernel(
                 )
                 for a in range(PASSES)
             ]
-            passes = [tok_pass] + tab_passes if j0 == 0 else tab_passes + [tok_pass]
-            acc = psum.tile([P, BANK], F32, name="acc")
+            passes = tab_passes[:-1] + [tok_pass, tab_passes[-1]]
+            acc = psum.tile([P, BANK], F32, name="h_acc", bufs=2)
             for n, (lhs, lhs_scale, rhs, rhs_scale) in enumerate(passes):
                 nc.tensor.matmul_mx(
                     out=acc[:], lhsT=lhs, lhsT_scale=lhs_scale, rhs=rhs, rhs_scale=rhs_scale,
@@ -177,29 +196,38 @@ def tile_list_completion_popup_scores_kernel(
             nc.vector.tensor_tensor(page[b][:].indirect(places), h_part, wgs_sb[:, j0 : j0 + width], MULT)
 
         def replace_columns(b):
-            h_sb = keep.tile([P, S], F32, name=f"h{b}")
+            h_sb = relay.tile([P, S], F32, name=f"h{b}", offset=ROWS_BYTES * (b % 2), align_bytes=64)
             for j0 in range(0, S, BANK):
                 first_stage(b, j0, h_sb[:, j0 : j0 + BANK])
             put(b, 0, h_sb[:])
 
-        def fetch_contexts(b):
-            picked = keep.tile([P, CTX], F32, name="picked", tag="chain4", align_bytes=64)
-            nc.vector.tensor_copy(picked[:], page[b][:].indirect(list4[:]))
-            x_rows = keep.tile([P, CTX], BF16, name=f"x_rows{b}")
-            nc.vector.tensor_scalar(x_rows[:], picked[:], lim_sb[:, b : b + 1], None, MIN)
-            nc.sync.dma_start(x_planes[QUAD * b : QUAD * (b + 1), :, :], x_rows[:])
+        def pick(b, cols, tag):
+            picked = keep.tile([P, cols.stop - cols.start], F32, name=f"picked{b}", tag=tag, align_bytes=64)
+            picks = list4[:, cols.start // LANES : cols.stop // LANES]
+            nc.vector.tensor_copy(picked[:], page[b][:].indirect(picks))
+            return picked
 
-        for j0, tag in ((0, "h0_first"), (BANK, "chain4")):
-            h_part = keep.tile([P, BANK], F32, name=f"h0_{j0}", tag=tag, align_bytes=64)
+        def limit(b, picked, x_rows, cols):
+            nc.vector.tensor_scalar(x_rows[:], picked[:], lim_sb[:, b : b + 1], None, MIN)
+            nc.sync.dma_start(x_planes[QUAD * b : QUAD * (b + 1), :, cols], x_rows[:])
+
+        for j0 in range(0, S, BANK):
+            h_part = keep.tile([P, BANK], F32, name=f"h0_{j0}")
             first_stage(0, j0, h_part[:])
             put(0, j0, h_part[:])
-        replace_columns(1)
-        w1_q.append(quantise_w1(1, "chain4"))
-        fetch_contexts(0)
-        fetch_contexts(1)
-        for b in range(2, BLOCKS):
-            replace_columns(b)
-            fetch_contexts(b)
+        held = relay.tile([P, W_COLS, PACK], BF16, name="w1_woven_relay", offset=ROWS_BYTES, align_bytes=64)
+        w1_q.append(quantise_w1(1, [woven_tile("woven_a"), held, woven_tile("picked0")]))
+        every = slice(0, CTX)
+        for b in range(BLOCKS - 1):
+            picked = pick(b, every, f"picked{b % 2}")
+            replace_columns(b + 1)
+            x_rows = relay.tile([P, CTX], BF16, name=f"x_rows{b}", offset=H_BYTES * (1 - b % 2), align_bytes=64)
+            limit(b, picked, x_rows, every)
+        halves = [slice(0, CTX // 2), slice(CTX // 2, CTX)]
+        for cols in halves:
+            picked = pick(BLOCKS - 1, cols, "picked1")
+            x_rows = keep.tile([P, CTX // 2], BF16, name=f"x_last{cols.start}")
+            limit(BLOCKS - 1, picked, x_rows, cols)
 
         def gather_candidates(half, tag):
             tile = keep.tile([P, BANK], U32, name=f"v2_words{half}", tag=tag, align_bytes=64)
@@ -207,23 +235,33 @@ def tile_list_completion_popup_scores_kernel(
             nc.vector.tensor_copy(tile[:], tab2_sb[:].indirect(picks))
             return tile
 
-        v2_words = [gather_candidates(0, "chain4")]
+        v2_words = [gather_candidates(0, "picked1")]
         x_woven = keep.tile([P, CTX, PACK], BF16, tag="woven", align_bytes=64)
-        nc.vector.tensor_copy(
-            x_woven[:].rearrange("p (c i) t -> p c t i", i=4),
-            x_planes[:].rearrange("p t (c i) -> p c t i", i=4),
-        )
         x_codes = keep.tile([P, CTX], U32, align_bytes=64)
         x_plane = keep.tile([P, CTX], U8, align_bytes=64)
-        nc.vector.quantize_mx(
-            out=x_codes[:].bitcast(FP8X4), scales=x_plane[:],
-            in_=x_woven[:].rearrange("p c t -> p (c t)"),
-        )
+
+        def weave(copy, cols):
+            copy(
+                x_woven[:, cols, :].rearrange("p (c i) t -> p c t i", i=4),
+                x_planes[:, :, cols].rearrange("p t (c i) -> p c t i", i=4),
+            )
+
+        def quantise_x(cols):
+            nc.vector.quantize_mx(
+                out=x_codes[:, cols].bitcast(FP8X4), scales=x_plane[:, cols],
+                in_=x_woven[:, cols, :].rearrange("p c t -> p (c t)"),
+            )
+
+        weave(nc.vector.tensor_copy, halves[0])
+        weave(nc.scalar.copy, slice(WEAVE_SPLIT, CTX))
+        quantise_x(halves[0])
+        weave(nc.vector.tensor_copy, slice(CTX // 2, WEAVE_SPLIT))
+        quantise_x(halves[1])
         v2_words.append(gather_candidates(1, "woven"))
 
         for c in range(S2 // P):
             half, u = divmod(c, 4)
-            acc = psum.tile([P, BANK], F32, name="acc")
+            acc = psum.tile([P, BANK], F32, name="e_acc", bufs=6)
             nc.tensor.matmul_mx(
                 out=acc[:],
                 lhsT=v2_words[half][:, u * P : (u + 1) * P].bitcast(FP8X4),
@@ -232,6 +270,9 @@ def tile_list_completion_popup_scores_kernel(
                 start=True, stop=True,
             )
             score = ring.tile([P, CTX], F32, name="score")
-            nc.scalar.activation(score[:], acc[:], TANH)
-            nc.vector.tensor_tensor(fit_sb[half][:, u, :], score[:], fit_sb[half][:, u, :], MULT)
-            nc.sync.dma_start(out[c * P : (c + 1) * P, :], fit_sb[half][:, u, :])
+            step = CTX // 2 if c == S2 // P - 1 else CTX
+            for j0 in range(0, CTX, step):
+                cols = slice(j0, j0 + step)
+                nc.scalar.activation(score[:, cols], acc[:, cols], TANH)
+                nc.vector.tensor_tensor(fit_sb[half][:, u, cols], score[:, cols], fit_sb[half][:, u, cols], MULT)
+                nc.sync.dma_start(out[c * P : (c + 1) * P, cols], fit_sb[half][:, u, cols])

from contextlib import ExitStack

import concourse.mybir as mybir

K, M, H, T, S, T2, S2, T3, CTX = 1536, 512, 512, 4096, 1024, 2048, 1024, 4096, 512
FLOPS = 2 * (K + M) * H * S + 2 * H * S2 * CTX

F32 = mybir.dt.float32
BF16 = mybir.dt.bfloat16
I32 = mybir.dt.int32
U32 = mybir.dt.uint32
U16 = mybir.dt.uint16
U8 = mybir.dt.uint8
FP8X4 = mybir.dt.float8_e4m3fn_x4
FP4X4 = mybir.dt.float4_e2m1fn_x4
MULT = mybir.AluOpType.mult
MIN = mybir.AluOpType.min
TANH = mybir.ActivationFunctionType.Tanh

P = 128
PACK = 4
QUADS = 4
QUAD = P // QUADS
K_PASS = P * PACK
PASSES = K // K_PASS
BLOCKS = H // P
BANK = 512
LANES = 16
W_COLS = H // 2
WEAVE_SPLIT = 368
ROWS_BYTES = 2 * CTX
H_BYTES = 4 * S


def tile_list_completion_popup_scores_kernel(
    tc, tab_words, tab_scales, offs, tab2_words, tab2_scales, offs2, offs3, offs4,
    tok_words, tok_scales, w4_words, w4_scales, w1, wgs, page0, lim, fit, out,
):
    nc = tc.nc

    def words_of(dram, a):
        return dram[a].rearrange("p n t -> p (n t)").bitcast(I32)

    with ExitStack() as ctx:
        keep = ctx.enter_context(tc.tile_pool(name="keep", bufs=1))
        ring = ctx.enter_context(tc.tile_pool(name="ring", bufs=4))
        relay = ctx.enter_context(tc.tile_pool(name="relay", bufs=1))
        psum = ctx.enter_context(tc.psum_pool(name="psum", bufs=1))

        def load_list(dram, name):
            tile = keep.tile(list(dram.shape), U16, name=name)
            nc.sync.dma_start(tile[:], dram)
            return tile

        def load_scale_rows(plane, dram):
            for r in range(4):
                nc.sync.dma_start(plane[r::QUAD, :].bitcast(I32), dram[0, r::4, :].bitcast(I32))

        def load_packed_scale_rows(plane, dram):
            for q in (0, 2, 1, 3):
                rows = slice(QUAD * q, QUAD * q + 4 * PASSES)
                nc.gpsimd.dma_start(plane[rows, :].bitcast(I32), dram[:, 4 * q : 4 * q + 4, :].bitcast(I32))

        tab_plane = keep.tile([P, T], U8, tag="chain3", align_bytes=64)
        nc.gpsimd.memset(tab_plane[:].bitcast(I32), 0)
        load_packed_scale_rows(tab_plane, tab_scales)
        tab2_plane = keep.tile([P, T3], U8, tag="chain1", align_bytes=64)
        nc.vector.memset(tab2_plane[:].bitcast(I32), 0)

        def load_w1(half):
            raws = []
            for a in range(PASSES):
                raw = keep.tile([P, PACK, W_COLS], F32, name=f"w1_raw{half}{a}")
                rows = w1[a * K_PASS : (a + 1) * K_PASS, half * W_COLS : (half + 1) * W_COLS]
                nc.sync.dma_start(raw[:], rows.rearrange("(p t) c -> p t c", t=PACK))
                raws.append(raw)
            return raws

        def load_page(b):
            tile = keep.tile([P, T2], F32, name=f"page{b}")
            nc.sync.dma_start(tile[:], page0[b * P : (b + 1) * P, :])
            return tile

        def table_tile(a):
            return keep.tile([P, T], U32, name=f"tab{a}", tag=f"tab{a}", align_bytes=64)

        def load_table(a, c0, c1):
            nc.sync.dma_start(tab_sb[a][:, c0:c1].bitcast(I32), words_of(tab_words, a)[:, c0:c1])

        def load_tok(part):
            tile = keep.tile([P, BANK], U32, name=f"tok{part}", align_bytes=64)
            nc.sync.dma_start(tile[:].bitcast(I32), words_of(tok_words, 0)[:, part * BANK : (part + 1) * BANK])
            return tile

        tab_sb = [table_tile(a) for a in range(PASSES)]
        w1_raw = [load_w1(0)]
        list1 = load_list(offs, "list1")
        tok_plane = keep.tile([P, S], U8, align_bytes=64)
        load_scale_rows(tok_plane, tok_scales)
        load_table(0, 0, T)
        list2 = load_list(offs2, "list2")
        list3 = load_list(offs3, "list3")
        load_scale_rows(tab2_plane, tab2_scales)
        load_table(1, 0, T)
        w4_plane = keep.tile([P, H], U8, align_bytes=64)
        load_scale_rows(w4_plane, w4_scales)
        load_table(2, 0, T)
        w4_sb = keep.tile([P, 2 * H], U8, align_bytes=64)
        nc.sync.dma_start(w4_sb[:].bitcast(I32), w4_words[0].bitcast(I32))
        tok_sb = [load_tok(0)]
        wgs_sb = keep.tile([P, S], F32)
        nc.sync.dma_start(wgs_sb[:, :BANK], wgs[:, :BANK])
        page = [load_page(0)]
        tok_sb.append(load_tok(1))
        nc.sync.dma_start(wgs_sb[:, BANK:], wgs[:, BANK:])
        w1_raw.append(load_w1(1))
        list4 = load_list(offs4, "list4")
        page.append(load_page(1))
        lim_sb = keep.tile([P, BLOCKS], F32)
        with nc.allow_non_contiguous_dma(reason="one ceiling for each partition and row block"):
            nc.sync.dma_start(lim_sb[:], lim.rearrange("(b p) -> p b", p=P))
        for b in range(2, BLOCKS):
            page.append(load_page(b))
        tab2_sb = keep.tile([P, T3], U32)
        nc.sync.dma_start(tab2_sb[:].bitcast(I32), words_of(tab2_words, 0))
        fit_sb = []
        for half in range(2):
            tile = keep.tile([P, 4, CTX], F32, name=f"fit{half}")
            rows = fit[half * 4 * P : (half + 1) * 4 * P, :]
            nc.sync.dma_start(tile[:], rows.rearrange("(c p) j -> p c j", p=P))
            fit_sb.append(tile)

        def quantise_w1(half, wovens):
            made = []
            for a, woven in enumerate(wovens):
                nc.scalar.copy(woven[:], w1_raw[half][a][:].rearrange("p t c -> p c t"))
                codes = keep.tile([P, W_COLS], U32, name=f"w1_codes{half}{a}", align_bytes=64)
                plane = keep.tile([P, W_COLS], U8, name=f"w1_plane{half}{a}", align_bytes=64)
                nc.vector.quantize_mx(
                    out=codes[:].bitcast(FP8X4), scales=plane[:],
                    in_=woven[:].rearrange("p c t -> p (c t)"),
                )
                made.append((codes, plane))
            return made

        def woven_tile(tag):
            return keep.tile([P, W_COLS, PACK], BF16, name="w1_woven", tag=tag, align_bytes=64)

        w1_q = [quantise_w1(0, [woven_tile(tag) for tag in ("woven_a", "woven_b", "woven_c")])]

        def gather_words(a, step, tag):
            tile = keep.tile([P, S], U32, name=f"v_words{a}", tag=tag, align_bytes=64)
            for j0 in range(0, S, step):
                picks = list1[:, j0 // LANES : (j0 + step) // LANES]
                nc.vector.tensor_copy(tile[:, j0 : j0 + step], tab_sb[a][:].indirect(picks))
            return tile

        v_words = [gather_words(0, S, "v_words0")]
        v2_plane = keep.tile([P, S2], U8, tag="tab0", align_bytes=64)
        nc.vector.tensor_copy(v2_plane[:], tab2_plane[:].indirect(list2[:]))
        v_words.append(gather_words(1, S, "chain1"))
        v_plane = keep.tile([P, S], U8, tag="tab1", align_bytes=64)
        for j0 in range(0, S, BANK):
            picks = list1[:, j0 // LANES : (j0 + BANK) // LANES]
            nc.vector.tensor_copy(v_plane[:, j0 : j0 + BANK], tab_plane[:].indirect(picks))
        v_words.append(gather_words(2, BANK, "chain3"))

        x_planes = keep.tile([P, PACK, CTX], BF16)

        def first_stage(b, j0, h_part):
            half, c0 = divmod(b * P, W_COLS)
            cols = slice(j0, j0 + BANK)
            tok_pass = (
                w4_sb[:, 2 * b * P : 2 * (b + 1) * P].bitcast(FP4X4), w4_plane[:, b * P : (b + 1) * P],
                tok_sb[j0 // BANK][:].bitcast(FP8X4), tok_plane[:, cols],
            )
            tab_passes = [
                (
                    w1_q[half][a][0][:, c0 : c0 + P].bitcast(FP8X4), w1_q[half][a][1][:, c0 : c0 + P],
                    v_words[a][:, cols].bitcast(FP8X4), v_plane[4 * a :, cols],
                )
                for a in range(PASSES)
            ]
            passes = tab_passes[:-1] + [tok_pass, tab_passes[-1]]
            acc = psum.tile([P, BANK], F32, name="h_acc", bufs=2)
            for n, (lhs, lhs_scale, rhs, rhs_scale) in enumerate(passes):
                nc.tensor.matmul_mx(
                    out=acc[:], lhsT=lhs, lhsT_scale=lhs_scale, rhs=rhs, rhs_scale=rhs_scale,
                    start=(n == 0), stop=(n == len(passes) - 1),
                )
            nc.scalar.copy(h_part, acc[:])

        def put(b, j0, h_part):
            width = h_part.shape[1]
            places = list3[:, j0 // LANES : (j0 + width) // LANES]
            nc.vector.tensor_tensor(page[b][:].indirect(places), h_part, wgs_sb[:, j0 : j0 + width], MULT)

        def replace_columns(b):
            h_sb = relay.tile([P, S], F32, name=f"h{b}", offset=ROWS_BYTES * (b % 2), align_bytes=64)
            for j0 in range(0, S, BANK):
                first_stage(b, j0, h_sb[:, j0 : j0 + BANK])
            put(b, 0, h_sb[:])

        def pick(b, cols, tag):
            picked = keep.tile([P, cols.stop - cols.start], F32, name=f"picked{b}", tag=tag, align_bytes=64)
            picks = list4[:, cols.start // LANES : cols.stop // LANES]
            nc.vector.tensor_copy(picked[:], page[b][:].indirect(picks))
            return picked

        def limit(b, picked, x_rows, cols):
            nc.vector.tensor_scalar(x_rows[:], picked[:], lim_sb[:, b : b + 1], None, MIN)
            nc.sync.dma_start(x_planes[QUAD * b : QUAD * (b + 1), :, cols], x_rows[:])

        for j0 in range(0, S, BANK):
            h_part = keep.tile([P, BANK], F32, name=f"h0_{j0}")
            first_stage(0, j0, h_part[:])
            put(0, j0, h_part[:])
        held = relay.tile([P, W_COLS, PACK], BF16, name="w1_woven_relay", offset=ROWS_BYTES, align_bytes=64)
        w1_q.append(quantise_w1(1, [woven_tile("woven_a"), held, woven_tile("picked0")]))
        every = slice(0, CTX)
        for b in range(BLOCKS - 1):
            picked = pick(b, every, f"picked{b % 2}")
            replace_columns(b + 1)
            x_rows = relay.tile([P, CTX], BF16, name=f"x_rows{b}", offset=H_BYTES * (1 - b % 2), align_bytes=64)
            limit(b, picked, x_rows, every)
        halves = [slice(0, CTX // 2), slice(CTX // 2, CTX)]
        for cols in halves:
            picked = pick(BLOCKS - 1, cols, "picked1")
            x_rows = keep.tile([P, CTX // 2], BF16, name=f"x_last{cols.start}")
            limit(BLOCKS - 1, picked, x_rows, cols)

        def gather_candidates(half, tag):
            tile = keep.tile([P, BANK], U32, name=f"v2_words{half}", tag=tag, align_bytes=64)
            picks = list2[:, half * BANK // LANES : (half + 1) * BANK // LANES]
            nc.vector.tensor_copy(tile[:], tab2_sb[:].indirect(picks))
            return tile

        v2_words = [gather_candidates(0, "picked1")]
        x_woven = keep.tile([P, CTX, PACK], BF16, tag="woven", align_bytes=64)
        x_codes = keep.tile([P, CTX], U32, align_bytes=64)
        x_plane = keep.tile([P, CTX], U8, align_bytes=64)

        def weave(copy, cols):
            copy(
                x_woven[:, cols, :].rearrange("p (c i) t -> p c t i", i=4),
                x_planes[:, :, cols].rearrange("p t (c i) -> p c t i", i=4),
            )

        def quantise_x(cols):
            nc.vector.quantize_mx(
                out=x_codes[:, cols].bitcast(FP8X4), scales=x_plane[:, cols],
                in_=x_woven[:, cols, :].rearrange("p c t -> p (c t)"),
            )

        weave(nc.vector.tensor_copy, halves[0])
        weave(nc.scalar.copy, slice(WEAVE_SPLIT, CTX))
        quantise_x(halves[0])
        weave(nc.vector.tensor_copy, slice(CTX // 2, WEAVE_SPLIT))
        quantise_x(halves[1])
        v2_words.append(gather_candidates(1, "woven"))

        for c in range(S2 // P):
            half, u = divmod(c, 4)
            acc = psum.tile([P, BANK], F32, name="e_acc", bufs=6)
            nc.tensor.matmul_mx(
                out=acc[:],
                lhsT=v2_words[half][:, u * P : (u + 1) * P].bitcast(FP8X4),
                lhsT_scale=v2_plane[:, c * P : (c + 1) * P],
                rhs=x_codes[:].bitcast(FP8X4), rhs_scale=x_plane[:],
                start=True, stop=True,
            )
            score = ring.tile([P, CTX], F32, name="score")
            step = CTX // 2 if c == S2 // P - 1 else CTX
            for j0 in range(0, CTX, step):
                cols = slice(j0, j0 + step)
                nc.scalar.activation(score[:, cols], acc[:, cols], TANH)
                nc.vector.tensor_tensor(fit_sb[half][:, u, cols], score[:, cols], fit_sb[half][:, u, cols], MULT)
                nc.sync.dma_start(out[c * P : (c + 1) * P, cols], fit_sb[half][:, u, cols])
